import numpy as np
import ml_dtypes


def mxq(x, axis, fmt="e4m3"):
    dtype, down = {"e4m3": (ml_dtypes.float8_e4m3fn, 7), "e5m2": (ml_dtypes.float8_e5m2, 14)}[fmt]
    v = np.moveaxis(np.asarray(x, np.float32).astype(ml_dtypes.bfloat16).astype(np.float64), axis, -1)
    blocks = v.reshape(v.shape[:-1] + (-1, 32))
    amax = np.abs(blocks).max(-1, keepdims=True)
    byte = np.maximum(np.where(amax > 0, np.frexp(amax)[1] - 1 + 127, 0) - down, 1)
    scale = np.exp2(byte - 127.0)
    codes = (blocks / scale).astype(np.float32).astype(dtype).astype(np.float64)
    return np.moveaxis((codes * scale).reshape(v.shape), -1, axis)


WIDE = False


def mx_kscale(k):
    if not WIDE:
        return np.ones(k)
    levels = np.array([10, -10, 5, -5, 0])
    if k % 512:
        return np.exp2(np.random.permutation(np.resize(levels, k // 32))).repeat(32)
    a = np.empty((k // 512, 16))
    for p in range(k // 512):
        a[p, :8] = np.random.permutation(np.resize(levels, 8))
        for g in range(8):
            far = levels[np.abs(levels - a[p, g]) >= 10]
            a[p, g + 8] = far[np.random.randint(len(far))]
    return np.exp2(a.ravel()).repeat(32)


def f64(x):
    return np.asarray(x).astype(np.float64)


def striped(idx):
    return np.tile(idx.reshape(-1, 16).T, (8, 1)).astype(np.uint16)


def unstriped(offs):
    return offs[:16].T.reshape(-1).astype(np.int64)


E2M1 = np.array([0.0, 0.5, 1.0, 1.5, 2.0, 3.0, 4.0, 6.0, -0.0, -0.5, -1.0, -1.5, -2.0, -3.0, -4.0, -6.0])


def pack_weight(w, fmt):
    k, n = w.shape
    w = f64(np.asarray(w, np.float32).astype(ml_dtypes.bfloat16)).reshape(k // 32, 32, n)
    amax = np.abs(w).max(1)
    if fmt == "e4m3":
        byte = np.frexp(amax)[1] - 1 + 127 - 7
    else:
        mant, ex = np.frexp(amax / 6.0)
        byte = np.where(mant > 0.5, ex, ex - 1) + 127
    byte = np.clip(np.where(amax > 0, byte, 1), 1, 254)
    scaled = (w * np.exp2(127.0 - byte)[:, None, :]).reshape(k, n).astype(np.float32)
    by_word = np.ascontiguousarray(scaled.reshape(k // 512, 128, 4, n).transpose(0, 1, 3, 2))
    if fmt == "e4m3":
        words = by_word.astype(ml_dtypes.float8_e4m3fn).view(np.uint8)
    else:
        c = by_word.astype(ml_dtypes.float4_e2m1fn).view(np.uint8) & 0xF
        words = (c[..., 0::2] | (c[..., 1::2] << 4)).reshape(k // 512, 128, 2 * n)
    return np.ascontiguousarray(words), np.ascontiguousarray(byte.astype(np.uint8).reshape(k // 512, 16, n))


def unpack_weight(words, scales, fmt):
    g, _, n = scales.shape
    words = np.ascontiguousarray(words).reshape(g, 128, n, -1)
    if fmt == "e4m3":
        vals = words.view(ml_dtypes.float8_e4m3fn).astype(np.float64)
    else:
        nib = np.empty((g, 128, n, 4), np.uint8)
        nib[..., 0::2] = words & 0xF
        nib[..., 1::2] = words >> 4
        vals = E2M1[nib]
    vals = vals * np.repeat(np.exp2(scales.astype(np.float64) - 127.0), 8, axis=1)[..., None]
    return vals.transpose(0, 1, 3, 2).reshape(g * 512, n)


def gelu(v):
    return 0.5 * v * (1.0 + np.tanh(np.sqrt(2.0 / np.pi) * (v + 0.044715 * v**3)))


K, T, S, H, T3, S2, P = 1024, 4096, 1024, 1024, 2048, 512, 512

def setup_inputs():
    n = np.random.standard_normal
    s = mx_kscale(K)[:, None]
    u = mx_kscale(H)[:, None]
    tab_words, tab_scales = pack_weight(n((K, T)) * s, "e4m3")
    tab2_words, tab2_scales = pack_weight(n((H, T3)) / np.sqrt(H) / u, "e4m3")
    w4_words, w4_scales = pack_weight(0.7 * n((K, H)) / np.sqrt(K) / s, "e2m1")
    w2 = (0.7 * n((K, H)) / np.sqrt(K) / s).astype(np.float32)
    gain = (np.exp(0.3 * n(H)) * u[:, 0]).astype(np.float32)
    exper = np.exp(0.4 * n(S2)).astype(np.float32)
    return {"tab_words": tab_words, "tab_scales": tab_scales,
            "offs": striped(np.random.permutation(T)[:S]),
            "tab2_words": tab2_words, "tab2_scales": tab2_scales,
            "offs2": striped(np.random.permutation(T3)[:S2]),
            "pos1": striped(np.random.permutation(S)[:P]),
            "pos2": striped(np.random.permutation(S)[:P]),
            "w4_words": w4_words, "w4_scales": w4_scales,
            "w2": w2, "gain": gain, "exper": exper}

def reference(tab_words, tab_scales, offs, tab2_words, tab2_scales, offs2, pos1, pos2,
              w4_words, w4_scales, w2, gain, exper):
    v = unpack_weight(tab_words, tab_scales, "e4m3")[:, unstriped(offs)]
    v2 = unpack_weight(tab2_words, tab2_scales, "e4m3")[:, unstriped(offs2)]
    w1 = unpack_weight(w4_words, w4_scales, "e2m1")
    w2q = mxq(f64(w2), 0, "e4m3")
    first = w1.T @ v
    second = w2q.T @ v
    h = f64(gain)[:, None] * (np.maximum(first, second) + first)
    x1 = mxq(h[:, unstriped(pos1)], 0, "e4m3")
    x2 = mxq(np.abs(h[:, unstriped(pos2)]), 0, "e4m3")
    e1 = v2.T @ x1
    e2 = v2.T @ x2
    return e1 * e2 * f64(exper)[:, None]

@@ -1,0 +1,259 @@
+from contextlib import ExitStack
+
+import concourse.mybir as mybir
+from concourse.masks import make_identity
+
+K, T, S, H, T3, S2, NP = 1024, 4096, 1024, 1024, 2048, 512, 512
+FLOPS = 2 * (2 * K * H * S + 2 * H * S2 * NP)
+
+F32 = mybir.dt.float32
+BF16 = mybir.dt.bfloat16
+I32 = mybir.dt.int32
+U32 = mybir.dt.uint32
+U16 = mybir.dt.uint16
+U8 = mybir.dt.uint8
+FP8X4 = mybir.dt.float8_e4m3fn_x4
+FP4X4 = mybir.dt.float4_e2m1fn_x4
+ALU = mybir.AluOpType
+ACT = mybir.ActivationFunctionType
+
+P = 128
+PACK = 4
+BANK = 512
+HALF = 256
+KB = 1024
+
+
+def tile_list_safari_guide_match_kernel(
+    tc, tab_words, tab_scales, offs, tab2_words, tab2_scales, offs2, pos1, pos2,
+    w4_words, w4_scales, w2, gain, exper, out,
+):
+    nc = tc.nc
+    with ExitStack() as ctx:
+        keep = ctx.enter_context(tc.tile_pool(name="keep", bufs=1))
+        shared = ctx.enter_context(tc.tile_pool(name="shared", bufs=1))
+        ring = ctx.enter_context(tc.tile_pool(name="ring", bufs=3))
+        psum = ctx.enter_context(tc.psum_pool(name="psum", bufs=4))
+
+        def kept(shape, dtype, name):
+            return keep.tile(shape, dtype, name=name, align_bytes=64)
+
+        def placed(shape, name, offset):
+            return shared.tile(shape, F32, name=name, offset=offset)
+
+        def bank(shape, tag, name):
+            return psum.tile(shape, F32, name=name, tag=tag)
+
+        offs_sb = kept([P, S // 16], U16, "offs_sb")
+        offs2_sb = kept([P, S2 // 16], U16, "offs2_sb")
+        pos1_sb = kept([P, NP // 16], U16, "pos1_sb")
+        pos2_sb = kept([P, NP // 16], U16, "pos2_sb")
+        tab_w = [kept([P, T], U32, "tab_w%d" % a) for a in range(2)]
+        tab_s = kept([P, 2, T], U8, "tab_s")
+        tab2_w = [kept([P, T3], U32, "tab2_w%d" % a) for a in range(2)]
+        tab2_s = kept([P, T3], U8, "tab2_s")
+        w4_w = [kept([P, 2, 2 * BANK], U8, "w4_w%d" % b) for b in range(2)]
+        w4_s = kept([P, 2, H], U8, "w4_s")
+        gain_sb = kept([P, 2, PACK], F32, "gain_sb")
+        exper_sb = kept([P, S2 // P], F32, "exper_sb")
+        ident = kept([P, P], F32, "ident")
+        v_w = [kept([P, S], U32, "v_w%d" % a) for a in range(2)]
+        v_s = [kept([P, S], U8, "v_s%d" % a) for a in range(2)]
+        v2_w = [kept([P, S2], U32, "v2_w%d" % a) for a in range(2)]
+        v2_s = kept([P, S2], U8, "v2_s")
+        w2_c = [[kept([P, HALF], U32, "w2_c%d_%d" % (q, a)) for a in range(2)] for q in range(4)]
+        w2_s = [[kept([P, HALF], U8, "w2_s%d_%d" % (q, a)) for a in range(2)] for q in range(4)]
+
+        w2_raw = [[placed([P, PACK, HALF], "w2_raw%d_%d" % (q, a), (2 * q + a) * 4 * KB) for a in range(2)] for q in range(4)]
+        f_t = [[placed([P, 2, PACK, P], "f_t%d_%d" % (b, u), (32 + 16 * b + 4 * u) * KB) for u in range(4)] for b in range(2)]
+        m_t = [[placed([P, 2, PACK, P], "m_t%d_%d" % (b, u), (64 + 16 * b + 4 * u) * KB) for u in range(4)] for b in range(2)]
+
+        nc.vector.memset(tab_s[:].rearrange("p a t -> p (a t)").bitcast(I32), 0)
+        nc.gpsimd.memset(w4_s[:].rearrange("p a t -> p (a t)").bitcast(I32), 0)
+        nc.gpsimd.memset(tab2_s[:].bitcast(I32), 0)
+        make_identity(nc, ident[:])
+
+        def load_words(dst, src):
+            nc.sync.dma_start(out=dst[:].bitcast(I32), in_=src.rearrange("p t i -> p (t i)").bitcast(I32))
+
+        def load_w4(b):
+            nc.sync.dma_start(
+                out=w4_w[b][:].bitcast(I32),
+                in_=w4_words[:, :, 2 * BANK * b : 2 * BANK * (b + 1)].rearrange("a p c -> p a c").bitcast(I32),
+            )
+
+        def load_w2(q):
+            for a in range(2):
+                rows = w2[BANK * a : BANK * (a + 1), HALF * q : HALF * (q + 1)]
+                nc.sync.dma_start(out=w2_raw[q][a][:], in_=rows.rearrange("(p j) c -> p j c", j=PACK))
+
+        nc.sync.dma_start(offs_sb[:], offs)
+        nc.sync.dma_start(pos2_sb[:], pos2)
+        nc.sync.dma_start(pos1_sb[:], pos1)
+        nc.sync.dma_start(offs2_sb[:], offs2)
+        nc.scalar.dma_start(out=gain_sb[:], in_=gain.rearrange("(b p i) -> p b i", b=2, i=PACK))
+        load_words(tab_w[0], tab_words[0])
+        load_w4(0)
+        load_words(tab_w[1], tab_words[1])
+        for quad in range(4):
+            nc.scalar.dma_start(
+                out=tab_s[32 * quad : 32 * quad + 4, :, :].bitcast(I32),
+                in_=tab_scales[:, 4 * quad : 4 * quad + 4, :].rearrange("a r t -> r a t").bitcast(I32),
+            )
+        for quad in range(4):
+            nc.gpsimd.dma_start(
+                out=w4_s[32 * quad : 32 * quad + 4, :, :].bitcast(I32),
+                in_=w4_scales[:, 4 * quad : 4 * quad + 4, :].rearrange("a r t -> r a t").bitcast(I32),
+            )
+        load_w2(0)
+        load_w2(1)
+        load_w4(1)
+        load_w2(2)
+        load_w2(3)
+        for quad in range(4):
+            for a in range(2):
+                nc.sync.dma_start(
+                    out=tab2_s[32 * quad + 4 * a : 32 * quad + 4 * a + 4, :].bitcast(I32),
+                    in_=tab2_scales[a, 4 * quad : 4 * quad + 4, :].bitcast(I32),
+                )
+        load_words(tab2_w[0], tab2_words[0])
+        load_words(tab2_w[1], tab2_words[1])
+        with nc.allow_non_contiguous_dma(reason="one value of exper for each partition"):
+            nc.sync.dma_start(out=exper_sb[:], in_=exper.rearrange("(c p) -> p c", p=P))
+
+        nc.vector.tensor_copy(v_s[0][:], tab_s[:, 0, :].indirect(offs_sb[:]))
+        nc.vector.tensor_copy(v_w[0][:], tab_w[0][:].indirect(offs_sb[:]))
+        nc.vector.tensor_copy(v_s[1][:], tab_s[:, 1, :].indirect(offs_sb[:]))
+        for u in range(4):
+            nc.vector.tensor_copy(v_w[1][:, HALF * u : HALF * (u + 1)], tab_w[1][:].indirect(offs_sb[:, 16 * u : 16 * (u + 1)]))
+
+        def interleave(copy, dst, src):
+            copy(dst.rearrange("p (c i) j -> p c j i", i=4), src.rearrange("p j (c i) -> p c j i", i=4))
+
+        def abs_copy(dst, src):
+            nc.scalar.activation(out=dst, in_=src, func=ACT.Abs)
+
+        def first_products(b):
+            for n in range(8):
+                acc = bank([P, BANK], "mm" if (b == 1 or n < 4) else "tr", "f_acc")
+                cols = slice(P * n, P * (n + 1))
+                for a in range(2):
+                    nc.tensor.matmul_mx(
+                        out=acc[:], lhsT=v_w[a][:, cols].bitcast(FP8X4), lhsT_scale=v_s[a][:, cols],
+                        rhs=w4_w[b][:, a, :].bitcast(FP4X4), rhs_scale=w4_s[:, a, BANK * b : BANK * (b + 1)],
+                        start=(a == 0), stop=(a == 1),
+                    )
+                nc.scalar.activation(
+                    out=f_t[b][n // 2][:, n % 2, :, :], in_=acc[:].rearrange("p (m t) -> p t m", t=PACK), func=ACT.Copy
+                )
+
+        def quantise_w2(q, copy):
+            for a in range(2):
+                grouped = ring.tile([P, HALF, PACK], BF16, name="w2_grouped", align_bytes=64)
+                interleave(copy, grouped[:], w2_raw[q][a][:])
+                nc.vector.quantize_mx(
+                    out=w2_c[q][a][:].bitcast(FP8X4), scales=w2_s[q][a][:], in_=grouped[:].rearrange("p c j -> p (c j)")
+                )
+
+        def second_products(q):
+            b, hq = divmod(q, 2)
+            part = slice(64 * hq, 64 * (hq + 1))
+            for u in range(4):
+                acc = bank([P, 2, HALF], "mm", "s_acc")
+                for n2 in range(2):
+                    cols = slice(P * (2 * u + n2), P * (2 * u + n2 + 1))
+                    for a in range(2):
+                        nc.tensor.matmul_mx(
+                            out=acc[:, n2, :], lhsT=v_w[a][:, cols].bitcast(FP8X4), lhsT_scale=v_s[a][:, cols],
+                            rhs=w2_c[q][a][:].bitcast(FP8X4), rhs_scale=w2_s[q][a][:],
+                            start=(a == 0), stop=(a == 1),
+                        )
+                nc.vector.tensor_tensor(
+                    out=m_t[b][u][:, :, :, part], in0=acc[:].rearrange("p n (m t) -> p n t m", t=PACK),
+                    in1=f_t[b][u][:, :, :, part], op=ALU.max,
+                )
+
+        def h_tile(b, i):
+            h = placed([P, S], "h%d_%d" % (b, i), ((96 if b == 0 else 64) + 4 * i) * KB)
+            for half in range(2):
+                acc = bank([P, 4, P], "tr", "h_acc")
+                for step, src in enumerate((f_t, m_t)):
+                    for nn in range(4):
+                        n = 4 * half + nn
+                        nc.tensor.matmul(
+                            acc[:, nn, :], src[b][n // 2][:, n % 2, i, :], ident[:], is_transpose=True,
+                            start=(step == 0 and nn == 0), stop=(step == 1 and nn == 3),
+                        )
+                nc.scalar.activation(
+                    out=h[:, BANK * half : BANK * (half + 1)], in_=acc[:].rearrange("p n c -> p (n c)"),
+                    func=ACT.Copy, scale=gain_sb[:, b, i : i + 1],
+                )
+            return h
+
+        def quantise_x(picked, width, copy, name):
+            grouped = ring.tile([P, width, PACK], BF16, name="x_grouped", tag="x_grouped", align_bytes=64)
+            interleave(copy, grouped[:], picked[:])
+            codes = kept([P, width], U32, name + "_c")
+            scales = kept([P, width], U8, name + "_s")
+            nc.vector.quantize_mx(out=codes[:].bitcast(FP8X4), scales=scales[:], in_=grouped[:].rearrange("p c j -> p (c j)"))
+            return codes, scales
+
+        first_products(0)
+        for q in range(2):
+            quantise_w2(q, nc.vector.tensor_copy)
+            second_products(q)
+        pick2 = placed([P, PACK, NP], "pick2_0", 0)
+        pick1 = placed([P, PACK, NP], "pick1_0", 8 * KB)
+        for i in range(PACK):
+            h = h_tile(0, i)
+            nc.vector.tensor_copy(pick2[:, i, :], h[:].indirect(pos2_sb[:]))
+            nc.vector.tensor_copy(pick1[:, i, :], h[:].indirect(pos1_sb[:]))
+
+        first_products(1)
+        for q in range(2, 4):
+            quantise_w2(q, nc.scalar.copy)
+            second_products(q)
+        x2 = [quantise_x(pick2, NP, abs_copy, "x2_0")]
+        x1_0 = quantise_x(pick1, NP, nc.scalar.copy, "x1_0")
+
+        nc.vector.tensor_copy(v2_s[:], tab2_s[:].indirect(offs2_sb[:]))
+        for a in range(2):
+            nc.vector.tensor_copy(v2_w[a][:], tab2_w[a][:].indirect(offs2_sb[:]))
+
+        pick2 = placed([P, PACK, NP], "pick2_1", 16 * KB)
+        hs = []
+        for i in range(PACK):
+            hs.append(h_tile(1, i))
+            nc.vector.tensor_copy(pick2[:, i, :], hs[i][:].indirect(pos2_sb[:]))
+        x2.append(quantise_x(pick2, NP, abs_copy, "x2_1"))
+
+        def guide_pass(acc, c, a, codes, scales, start, stop):
+            cols = slice(P * c, P * (c + 1))
+            nc.tensor.matmul_mx(
+                out=acc, lhsT=v2_w[a][:, cols].bitcast(FP8X4), lhsT_scale=v2_s[4 * a : P, cols],
+                rhs=codes.bitcast(FP8X4), rhs_scale=scales, start=start, stop=stop,
+            )
+
+        e2 = placed([P, 4, NP], "e2", 32 * KB)
+        for c in range(4):
+            acc = bank([P, NP], "mm", "e2_acc")
+            for a in range(2):
+                guide_pass(acc[:], c, a, x2[a][0][:], x2[a][1][:], a == 0, a == 1)
+            nc.scalar.activation(out=e2[:, c, :], in_=acc[:], func=ACT.Copy, scale=exper_sb[:, c : c + 1])
+
+        for hf in range(2):
+            cols = slice(HALF * hf, HALF * (hf + 1))
+            pick1 = placed([P, PACK, HALF], "pick1_1_%d" % hf, (24 + 4 * hf) * KB)
+            for i in range(PACK):
+                nc.vector.tensor_copy(pick1[:, i, :], hs[i][:].indirect(pos1_sb[:, 16 * hf : 16 * (hf + 1)]))
+            x1_1 = quantise_x(pick1, HALF, nc.scalar.copy if hf == 0 else nc.vector.tensor_copy, "x1_1_%d" % hf)
+            for pair in range(2):
+                acc = bank([P, 2, HALF], "tr", "e1_acc")
+                for c2 in range(2):
+                    guide_pass(acc[:, c2, :], 2 * pair + c2, 0, x1_0[0][:, cols], x1_0[1][:, cols], c2 == 0, False)
+                for c2 in range(2):
+                    guide_pass(acc[:, c2, :], 2 * pair + c2, 1, x1_1[0][:], x1_1[1][:], False, c2 == 1)
+                res = placed([P, 2, HALF], "res%d_%d" % (hf, pair), (40 + 4 * hf + 2 * pair) * KB)
+                nc.vector.tensor_tensor(out=res[:], in0=acc[:], in1=e2[:, 2 * pair : 2 * pair + 2, cols], op=ALU.mult)
+                rows = out[HALF * pair : HALF * (pair + 1), cols]
+                nc.sync.dma_start(out=rows.rearrange("(c p) j -> p c j", p=P), in_=res[:])

@@ -23,6 +23,15 @@ BANK = 512
 HALF = 256
 KB = 1024
 
+TABLE = 0
+W4 = 32
+FIRST = 36
+LARGER = 68
+H0 = 100
+W2_WORK = 116
+PICKS = 136
+X_WORK = 152
+
 
 def tile_list_safari_guide_match_kernel(
     tc, tab_words, tab_scales, offs, tab2_words, tab2_scales, offs2, pos1, pos2,
@@ -32,14 +41,13 @@ def tile_list_safari_guide_match_kernel(
     with ExitStack() as ctx:
         keep = ctx.enter_context(tc.tile_pool(name="keep", bufs=1))
         shared = ctx.enter_context(tc.tile_pool(name="shared", bufs=1))
-        ring = ctx.enter_context(tc.tile_pool(name="ring", bufs=3))
         psum = ctx.enter_context(tc.psum_pool(name="psum", bufs=4))
 
         def kept(shape, dtype, name):
             return keep.tile(shape, dtype, name=name, align_bytes=64)
 
-        def placed(shape, name, offset):
-            return shared.tile(shape, F32, name=name, offset=offset)
+        def placed(shape, dtype, name, kib):
+            return shared.tile(shape, dtype, name=name, offset=kib * KB, align_bytes=64)
 
         def bank(shape, tag, name):
             return psum.tile(shape, F32, name=name, tag=tag)
@@ -48,84 +56,63 @@ def tile_list_safari_guide_match_kernel(
         offs2_sb = kept([P, S2 // 16], U16, "offs2_sb")
         pos1_sb = kept([P, NP // 16], U16, "pos1_sb")
         pos2_sb = kept([P, NP // 16], U16, "pos2_sb")
-        tab_w = [kept([P, T], U32, "tab_w%d" % a) for a in range(2)]
-        tab_s = kept([P, 2, T], U8, "tab_s")
-        tab2_w = [kept([P, T3], U32, "tab2_w%d" % a) for a in range(2)]
-        tab2_s = kept([P, T3], U8, "tab2_s")
-        w4_w = [kept([P, 2, 2 * BANK], U8, "w4_w%d" % b) for b in range(2)]
+        tab_w = [placed([P, T], U32, "tab_w%d" % a, TABLE + 16 * a) for a in range(2)]
+        tab_s = kept([P, T], U8, "tab_s")
+        w4_w = placed([P, 2, 2 * H], U8, "w4_w", W4)
         w4_s = kept([P, 2, H], U8, "w4_s")
         gain_sb = kept([P, 2, PACK], F32, "gain_sb")
         exper_sb = kept([P, S2 // P], F32, "exper_sb")
         ident = kept([P, P], F32, "ident")
         v_w = [kept([P, S], U32, "v_w%d" % a) for a in range(2)]
+        v_rows = kept([P, S], U8, "v_rows")
         v_s = [kept([P, S], U8, "v_s%d" % a) for a in range(2)]
-        v2_w = [kept([P, S2], U32, "v2_w%d" % a) for a in range(2)]
-        v2_s = kept([P, S2], U8, "v2_s")
-        w2_c = [[kept([P, HALF], U32, "w2_c%d_%d" % (q, a)) for a in range(2)] for q in range(4)]
         w2_s = [[kept([P, HALF], U8, "w2_s%d_%d" % (q, a)) for a in range(2)] for q in range(4)]
+        f_t = [[placed([P, 2, PACK, P], F32, "f_t%d_%d" % (b, u), FIRST + 16 * b + 4 * u) for u in range(4)] for b in range(2)]
+        m_t = [[placed([P, 2, PACK, P], F32, "m_t%d_%d" % (b, u), LARGER + 16 * b + 4 * u) for u in range(4)] for b in range(2)]
 
-        w2_raw = [[placed([P, PACK, HALF], "w2_raw%d_%d" % (q, a), (2 * q + a) * 4 * KB) for a in range(2)] for q in range(4)]
-        f_t = [[placed([P, 2, PACK, P], "f_t%d_%d" % (b, u), (32 + 16 * b + 4 * u) * KB) for u in range(4)] for b in range(2)]
-        m_t = [[placed([P, 2, PACK, P], "m_t%d_%d" % (b, u), (64 + 16 * b + 4 * u) * KB) for u in range(4)] for b in range(2)]
-
-        nc.vector.memset(tab_s[:].rearrange("p a t -> p (a t)").bitcast(I32), 0)
         nc.gpsimd.memset(w4_s[:].rearrange("p a t -> p (a t)").bitcast(I32), 0)
-        nc.gpsimd.memset(tab2_s[:].bitcast(I32), 0)
-        make_identity(nc, ident[:])
+        nc.vector.memset(tab_s[32:64, :].bitcast(I32), 0)
+        nc.vector.memset(tab_s[64:P, :].bitcast(I32), 0)
+        for a in range(2):
+            nc.vector.memset(v_s[a][:].bitcast(I32), 0)
 
         def load_words(dst, src):
             nc.sync.dma_start(out=dst[:].bitcast(I32), in_=src.rearrange("p t i -> p (t i)").bitcast(I32))
 
-        def load_w4(b):
-            nc.sync.dma_start(
-                out=w4_w[b][:].bitcast(I32),
-                in_=w4_words[:, :, 2 * BANK * b : 2 * BANK * (b + 1)].rearrange("a p c -> p a c").bitcast(I32),
-            )
-
-        def load_w2(q):
-            for a in range(2):
-                rows = w2[BANK * a : BANK * (a + 1), HALF * q : HALF * (q + 1)]
-                nc.sync.dma_start(out=w2_raw[q][a][:], in_=rows.rearrange("(p j) c -> p j c", j=PACK))
-
         nc.sync.dma_start(offs_sb[:], offs)
+        nc.sync.dma_start(out=tab_s[0:32, :].bitcast(I32), in_=tab_scales.rearrange("a q t -> (a q) t").bitcast(I32))
         nc.sync.dma_start(pos2_sb[:], pos2)
         nc.sync.dma_start(pos1_sb[:], pos1)
         nc.sync.dma_start(offs2_sb[:], offs2)
-        nc.scalar.dma_start(out=gain_sb[:], in_=gain.rearrange("(b p i) -> p b i", b=2, i=PACK))
         load_words(tab_w[0], tab_words[0])
-        load_w4(0)
+        nc.sync.dma_start(out=w4_w[:].bitcast(I32), in_=w4_words.rearrange("a p c -> p a c").bitcast(I32))
         load_words(tab_w[1], tab_words[1])
-        for quad in range(4):
-            nc.scalar.dma_start(
-                out=tab_s[32 * quad : 32 * quad + 4, :, :].bitcast(I32),
-                in_=tab_scales[:, 4 * quad : 4 * quad + 4, :].rearrange("a r t -> r a t").bitcast(I32),
-            )
         for quad in range(4):
             nc.gpsimd.dma_start(
                 out=w4_s[32 * quad : 32 * quad + 4, :, :].bitcast(I32),
                 in_=w4_scales[:, 4 * quad : 4 * quad + 4, :].rearrange("a r t -> r a t").bitcast(I32),
             )
-        load_w2(0)
-        load_w2(1)
-        load_w4(1)
-        load_w2(2)
-        load_w2(3)
-        for quad in range(4):
-            for a in range(2):
-                nc.sync.dma_start(
-                    out=tab2_s[32 * quad + 4 * a : 32 * quad + 4 * a + 4, :].bitcast(I32),
-                    in_=tab2_scales[a, 4 * quad : 4 * quad + 4, :].bitcast(I32),
-                )
-        load_words(tab2_w[0], tab2_words[0])
-        load_words(tab2_w[1], tab2_words[1])
+        nc.scalar.dma_start(out=gain_sb[:], in_=gain.rearrange("(b p i) -> p b i", b=2, i=PACK))
         with nc.allow_non_contiguous_dma(reason="one value of exper for each partition"):
-            nc.sync.dma_start(out=exper_sb[:], in_=exper.rearrange("(c p) -> p c", p=P))
+            nc.scalar.dma_start(out=exper_sb[:], in_=exper.rearrange("(c p) -> p c", p=P))
 
-        nc.vector.tensor_copy(v_s[0][:], tab_s[:, 0, :].indirect(offs_sb[:]))
+        nc.vector.tensor_copy(v_rows[:], tab_s[:].indirect(offs_sb[:]))
+        for a, queue in enumerate((nc.scalar, nc.gpsimd)):
+            for quad in range(4):
+                row = 16 * a + 4 * quad
+                queue.dma_start(
+                    out=v_s[a][32 * quad : 32 * quad + 4, :].bitcast(I32), in_=v_rows[row : row + 4, :].bitcast(I32)
+                )
+        make_identity(nc, ident[:])
         nc.vector.tensor_copy(v_w[0][:], tab_w[0][:].indirect(offs_sb[:]))
-        nc.vector.tensor_copy(v_s[1][:], tab_s[:, 1, :].indirect(offs_sb[:]))
         for u in range(4):
             nc.vector.tensor_copy(v_w[1][:, HALF * u : HALF * (u + 1)], tab_w[1][:].indirect(offs_sb[:, 16 * u : 16 * (u + 1)]))
+
+        w2_raw = [[placed([P, PACK, HALF], F32, "w2_raw%d_%d" % (q, a), TABLE + 8 * q + 4 * a) for a in range(2)] for q in range(4)]
+        for q in range(4):
+            for a in range(2):
+                rows = w2[BANK * a : BANK * (a + 1), HALF * q : HALF * (q + 1)]
+                nc.sync.dma_start(out=w2_raw[q][a][:], in_=rows.rearrange("(p j) c -> p j c", j=PACK))
 
         def interleave(copy, dst, src):
             copy(dst.rearrange("p (c i) j -> p c j i", i=4), src.rearrange("p j (c i) -> p c j i", i=4))
@@ -140,16 +127,19 @@ def tile_list_safari_guide_match_kernel(
                 for a in range(2):
                     nc.tensor.matmul_mx(
                         out=acc[:], lhsT=v_w[a][:, cols].bitcast(FP8X4), lhsT_scale=v_s[a][:, cols],
-                        rhs=w4_w[b][:, a, :].bitcast(FP4X4), rhs_scale=w4_s[:, a, BANK * b : BANK * (b + 1)],
+                        rhs=w4_w[:, a, 2 * BANK * b : 2 * BANK * (b + 1)].bitcast(FP4X4), rhs_scale=w4_s[:, a, BANK * b : BANK * (b + 1)],
                         start=(a == 0), stop=(a == 1),
                     )
                 nc.scalar.activation(
                     out=f_t[b][n // 2][:, n % 2, :, :], in_=acc[:].rearrange("p (m t) -> p t m", t=PACK), func=ACT.Copy
                 )
 
+        w2_c = [[] for q in range(4)]
+
         def quantise_w2(q, copy):
             for a in range(2):
-                grouped = ring.tile([P, HALF, PACK], BF16, name="w2_grouped", align_bytes=64)
+                w2_c[q].append(placed([P, HALF], U32, "w2_c%d_%d" % (q, a), W2_WORK + (4 * q + 2 * a if q < 2 else 4 + 2 * q + a)))
+                grouped = placed([P, HALF, PACK], BF16, "w2_grouped%d_%d" % (q, a), W2_WORK + (12 if q < 2 else -8) + 4 * q + 2 * a)
                 interleave(copy, grouped[:], w2_raw[q][a][:])
                 nc.vector.quantize_mx(
                     out=w2_c[q][a][:].bitcast(FP8X4), scales=w2_s[q][a][:], in_=grouped[:].rearrange("p c j -> p (c j)")
@@ -174,7 +164,7 @@ def tile_list_safari_guide_match_kernel(
                 )
 
         def h_tile(b, i):
-            h = placed([P, S], "h%d_%d" % (b, i), ((96 if b == 0 else 64) + 4 * i) * KB)
+            h = placed([P, S], F32, "h%d_%d" % (b, i), (H0 if b == 0 else LARGER) + 4 * i)
             for half in range(2):
                 acc = bank([P, 4, P], "tr", "h_acc")
                 for step, src in enumerate((f_t, m_t)):
@@ -190,10 +180,9 @@ def tile_list_safari_guide_match_kernel(
                 )
             return h
 
-        def quantise_x(picked, width, copy, name):
-            grouped = ring.tile([P, width, PACK], BF16, name="x_grouped", tag="x_grouped", align_bytes=64)
+        def quantise_x(picked, width, copy, name, grouped_at, codes):
+            grouped = placed([P, width, PACK], BF16, name + "_grouped", grouped_at)
             interleave(copy, grouped[:], picked[:])
-            codes = kept([P, width], U32, name + "_c")
             scales = kept([P, width], U8, name + "_s")
             nc.vector.quantize_mx(out=codes[:].bitcast(FP8X4), scales=scales[:], in_=grouped[:].rearrange("p c j -> p (c j)"))
             return codes, scales
@@ -202,30 +191,48 @@ def tile_list_safari_guide_match_kernel(
         for q in range(2):
             quantise_w2(q, nc.vector.tensor_copy)
             second_products(q)
-        pick2 = placed([P, PACK, NP], "pick2_0", 0)
-        pick1 = placed([P, PACK, NP], "pick1_0", 8 * KB)
-        for i in range(PACK):
+        pick2 = placed([P, PACK, NP], F32, "pick2_0", PICKS)
+        pick1 = placed([P, PACK, NP], F32, "pick1_0", PICKS + 8)
+
+        def pick_block0(i):
             h = h_tile(0, i)
             nc.vector.tensor_copy(pick2[:, i, :], h[:].indirect(pos2_sb[:]))
             nc.vector.tensor_copy(pick1[:, i, :], h[:].indirect(pos1_sb[:]))
 
+        pick_block0(0)
+        pick_block0(1)
         first_products(1)
         for q in range(2, 4):
             quantise_w2(q, nc.scalar.copy)
             second_products(q)
-        x2 = [quantise_x(pick2, NP, abs_copy, "x2_0")]
-        x1_0 = quantise_x(pick1, NP, nc.scalar.copy, "x1_0")
+        pick_block0(2)
+        pick_block0(3)
 
-        nc.vector.tensor_copy(v2_s[:], tab2_s[:].indirect(offs2_sb[:]))
+        tab2_w = [placed([P, T3], U32, "tab2_w%d" % a, TABLE + 8 * a) for a in range(2)]
+        tab2_s = placed([P, T3], U8, "tab2_s", W4)
+        nc.gpsimd.memset(tab2_s[:].bitcast(I32), 0)
+        for a in range(2):
+            load_words(tab2_w[a], tab2_words[a])
+        for quad in range(4):
+            for a in range(2):
+                nc.sync.dma_start(
+                    out=tab2_s[32 * quad + 4 * a : 32 * quad + 4 * a + 4, :].bitcast(I32),
+                    in_=tab2_scales[a, 4 * quad : 4 * quad + 4, :].bitcast(I32),
+                )
+        v2_w = [placed([P, S2], U32, "v2_w%d" % a, FIRST + 2 * a) for a in range(2)]
+        v2_s = placed([P, S2], U8, "v2_s", FIRST + 4)
         for a in range(2):
             nc.vector.tensor_copy(v2_w[a][:], tab2_w[a][:].indirect(offs2_sb[:]))
+        nc.vector.tensor_copy(v2_s[:], tab2_s[:].indirect(offs2_sb[:]))
 
-        pick2 = placed([P, PACK, NP], "pick2_1", 16 * KB)
+        x2_0 = quantise_x(pick2, NP, abs_copy, "x2_0", X_WORK, kept([P, NP], U32, "x2_0_c"))
+        x1_0 = quantise_x(pick1, NP, nc.scalar.copy, "x1_0", X_WORK + 4, placed([P, NP], U32, "x1_0_c", X_WORK + 12))
+
+        pick2_1 = placed([P, PACK, NP], F32, "pick2_1", TABLE + 16)
         hs = []
         for i in range(PACK):
             hs.append(h_tile(1, i))
-            nc.vector.tensor_copy(pick2[:, i, :], hs[i][:].indirect(pos2_sb[:]))
-        x2.append(quantise_x(pick2, NP, abs_copy, "x2_1"))
+            nc.vector.tensor_copy(pick2_1[:, i, :], hs[i][:].indirect(pos2_sb[:]))
 
         def guide_pass(acc, c, a, codes, scales, start, stop):
             cols = slice(P * c, P * (c + 1))
@@ -234,26 +241,35 @@ def tile_list_safari_guide_match_kernel(
                 rhs=codes.bitcast(FP8X4), rhs_scale=scales, start=start, stop=stop,
             )
 
-        e2 = placed([P, 4, NP], "e2", 32 * KB)
+        e2_acc = [bank([P, NP], "mm", "e2_acc") for c in range(4)]
         for c in range(4):
-            acc = bank([P, NP], "mm", "e2_acc")
-            for a in range(2):
-                guide_pass(acc[:], c, a, x2[a][0][:], x2[a][1][:], a == 0, a == 1)
-            nc.scalar.activation(out=e2[:, c, :], in_=acc[:], func=ACT.Copy, scale=exper_sb[:, c : c + 1])
+            guide_pass(e2_acc[c][:], c, 0, x2_0[0][:], x2_0[1][:], True, False)
+        e1_acc = [[bank([P, 2, HALF], "tr", "e1_acc") for pair in range(2)] for hf in range(2)]
+        for hf in range(2):
+            cols = slice(HALF * hf, HALF * (hf + 1))
+            for c in range(4):
+                guide_pass(e1_acc[hf][c // 2][:, c % 2, :], c, 0, x1_0[0][:, cols], x1_0[1][:, cols], c % 2 == 0, False)
+
+        x2_1 = quantise_x(pick2_1, NP, abs_copy, "x2_1", X_WORK + 8, kept([P, NP], U32, "x2_1_c"))
+        e2 = placed([P, 4, NP], F32, "e2", FIRST + 8)
+        for c in range(4):
+            guide_pass(e2_acc[c][:], c, 1, x2_1[0][:], x2_1[1][:], False, True)
+            nc.scalar.activation(out=e2[:, c, :], in_=e2_acc[c][:], func=ACT.Copy, scale=exper_sb[:, c : c + 1])
 
         for hf in range(2):
             cols = slice(HALF * hf, HALF * (hf + 1))
-            pick1 = placed([P, PACK, HALF], "pick1_1_%d" % hf, (24 + 4 * hf) * KB)
+            pick1_1 = placed([P, PACK, HALF], F32, "pick1_1_%d" % hf, X_WORK + 12 - 4 * hf)
             for i in range(PACK):
-                nc.vector.tensor_copy(pick1[:, i, :], hs[i][:].indirect(pos1_sb[:, 16 * hf : 16 * (hf + 1)]))
-            x1_1 = quantise_x(pick1, HALF, nc.scalar.copy if hf == 0 else nc.vector.tensor_copy, "x1_1_%d" % hf)
+                nc.vector.tensor_copy(pick1_1[:, i, :], hs[i][:].indirect(pos1_sb[:, 16 * hf : 16 * (hf + 1)]))
+            x1_1 = quantise_x(
+                pick1_1, HALF, nc.scalar.copy if hf == 0 else nc.vector.tensor_copy, "x1_1_%d" % hf,
+                X_WORK + 2 * hf, kept([P, HALF], U32, "x1_1_c%d" % hf),
+            )
             for pair in range(2):
-                acc = bank([P, 2, HALF], "tr", "e1_acc")
-                for c2 in range(2):
-                    guide_pass(acc[:, c2, :], 2 * pair + c2, 0, x1_0[0][:, cols], x1_0[1][:, cols], c2 == 0, False)
+                acc = e1_acc[hf][pair]
                 for c2 in range(2):
                     guide_pass(acc[:, c2, :], 2 * pair + c2, 1, x1_1[0][:], x1_1[1][:], False, c2 == 1)
-                res = placed([P, 2, HALF], "res%d_%d" % (hf, pair), (40 + 4 * hf + 2 * pair) * KB)
+                res = placed([P, 2, HALF], F32, "res%d_%d" % (hf, pair), FIRST + 16 + 4 * hf + 2 * pair)
                 nc.vector.tensor_tensor(out=res[:], in0=acc[:], in1=e2[:, 2 * pair : 2 * pair + 2, cols], op=ALU.mult)
                 rows = out[HALF * pair : HALF * (pair + 1), cols]
                 nc.sync.dma_start(out=rows.rearrange("(c p) j -> p c j", p=P), in_=res[:])

@@ -31,6 +31,7 @@ H0 = 100
 W2_WORK = 116
 PICKS = 136
 X_WORK = 152
+ROWS = 168
 
 
 def tile_list_safari_guide_match_kernel(
@@ -41,7 +42,7 @@ def tile_list_safari_guide_match_kernel(
     with ExitStack() as ctx:
         keep = ctx.enter_context(tc.tile_pool(name="keep", bufs=1))
         shared = ctx.enter_context(tc.tile_pool(name="shared", bufs=1))
-        psum = ctx.enter_context(tc.psum_pool(name="psum", bufs=4))
+        psum = ctx.enter_context(tc.psum_pool(name="psum", bufs=8))
 
         def kept(shape, dtype, name):
             return keep.tile(shape, dtype, name=name, align_bytes=64)
@@ -49,30 +50,31 @@ def tile_list_safari_guide_match_kernel(
         def placed(shape, dtype, name, kib):
             return shared.tile(shape, dtype, name=name, offset=kib * KB, align_bytes=64)
 
-        def bank(shape, tag, name):
-            return psum.tile(shape, F32, name=name, tag=tag)
+        def bank(shape, name):
+            return psum.tile(shape, F32, name=name, tag="bank")
 
         offs_sb = kept([P, S // 16], U16, "offs_sb")
         offs2_sb = kept([P, S2 // 16], U16, "offs2_sb")
         pos1_sb = kept([P, NP // 16], U16, "pos1_sb")
         pos2_sb = kept([P, NP // 16], U16, "pos2_sb")
+        tab_s = placed([P, T], U8, "tab_s", TABLE + 16)
         tab_w = [placed([P, T], U32, "tab_w%d" % a, TABLE + 16 * a) for a in range(2)]
-        tab_s = kept([P, T], U8, "tab_s")
         w4_w = placed([P, 2, 2 * H], U8, "w4_w", W4)
         w4_s = kept([P, 2, H], U8, "w4_s")
-        gain_sb = kept([P, 2, PACK], F32, "gain_sb")
-        exper_sb = kept([P, S2 // P], F32, "exper_sb")
         ident = kept([P, P], F32, "ident")
         v_w = [kept([P, S], U32, "v_w%d" % a) for a in range(2)]
-        v_rows = kept([P, S], U8, "v_rows")
+        v_rows = placed([P, S], U8, "v_rows", ROWS)
+        tab2_s = kept([P, T3], U8, "tab2_s")
+        v2_rows = kept([P, S2], U8, "v2_rows")
         v_s = [kept([P, S], U8, "v_s%d" % a) for a in range(2)]
         w2_s = [[kept([P, HALF], U8, "w2_s%d_%d" % (q, a)) for a in range(2)] for q in range(4)]
         f_t = [[placed([P, 2, PACK, P], F32, "f_t%d_%d" % (b, u), FIRST + 16 * b + 4 * u) for u in range(4)] for b in range(2)]
         m_t = [[placed([P, 2, PACK, P], F32, "m_t%d_%d" % (b, u), LARGER + 16 * b + 4 * u) for u in range(4)] for b in range(2)]
 
         nc.gpsimd.memset(w4_s[:].rearrange("p a t -> p (a t)").bitcast(I32), 0)
-        nc.vector.memset(tab_s[32:64, :].bitcast(I32), 0)
-        nc.vector.memset(tab_s[64:P, :].bitcast(I32), 0)
+        for window in (tab_s, tab2_s):
+            nc.vector.memset(window[32:64, :].bitcast(I32), 0)
+            nc.vector.memset(window[64:P, :].bitcast(I32), 0)
         for a in range(2):
             nc.vector.memset(v_s[a][:].bitcast(I32), 0)
 
@@ -81,29 +83,34 @@ def tile_list_safari_guide_match_kernel(
 
         nc.sync.dma_start(offs_sb[:], offs)
         nc.sync.dma_start(out=tab_s[0:32, :].bitcast(I32), in_=tab_scales.rearrange("a q t -> (a q) t").bitcast(I32))
+        nc.sync.dma_start(offs2_sb[:], offs2)
+        nc.sync.dma_start(out=tab2_s[0:32, :].bitcast(I32), in_=tab2_scales.rearrange("a q t -> (a q) t").bitcast(I32))
         nc.sync.dma_start(pos2_sb[:], pos2)
         nc.sync.dma_start(pos1_sb[:], pos1)
-        nc.sync.dma_start(offs2_sb[:], offs2)
         load_words(tab_w[0], tab_words[0])
         nc.sync.dma_start(out=w4_w[:].bitcast(I32), in_=w4_words.rearrange("a p c -> p a c").bitcast(I32))
-        load_words(tab_w[1], tab_words[1])
         for quad in range(4):
-            nc.gpsimd.dma_start(
+            (nc.scalar if quad == 0 else nc.gpsimd).dma_start(
                 out=w4_s[32 * quad : 32 * quad + 4, :, :].bitcast(I32),
                 in_=w4_scales[:, 4 * quad : 4 * quad + 4, :].rearrange("a r t -> r a t").bitcast(I32),
             )
-        nc.scalar.dma_start(out=gain_sb[:], in_=gain.rearrange("(b p i) -> p b i", b=2, i=PACK))
-        with nc.allow_non_contiguous_dma(reason="one value of exper for each partition"):
-            nc.scalar.dma_start(out=exper_sb[:], in_=exper.rearrange("(c p) -> p c", p=P))
 
         nc.vector.tensor_copy(v_rows[:], tab_s[:].indirect(offs_sb[:]))
-        for a, queue in enumerate((nc.scalar, nc.gpsimd)):
+
+        def move_scale_rows(a):
             for quad in range(4):
                 row = 16 * a + 4 * quad
-                queue.dma_start(
+                nc.sync.dma_start(
                     out=v_s[a][32 * quad : 32 * quad + 4, :].bitcast(I32), in_=v_rows[row : row + 4, :].bitcast(I32)
                 )
+
+        move_scale_rows(0)
+        load_words(tab_w[1], tab_words[1])
+        move_scale_rows(1)
+        gain_sb = placed([P, 2, PACK], F32, "gain_sb", ROWS)
+        nc.gpsimd.dma_start(out=gain_sb[:], in_=gain.rearrange("(b p i) -> p b i", b=2, i=PACK))
         make_identity(nc, ident[:])
+        nc.vector.tensor_copy(v2_rows[:], tab2_s[:].indirect(offs2_sb[:]))
         nc.vector.tensor_copy(v_w[0][:], tab_w[0][:].indirect(offs_sb[:]))
         for u in range(4):
             nc.vector.tensor_copy(v_w[1][:, HALF * u : HALF * (u + 1)], tab_w[1][:].indirect(offs_sb[:, 16 * u : 16 * (u + 1)]))
@@ -120,9 +127,9 @@ def tile_list_safari_guide_match_kernel(
         def abs_copy(dst, src):
             nc.scalar.activation(out=dst, in_=src, func=ACT.Abs)
 
-        def first_products(b):
-            for n in range(8):
-                acc = bank([P, BANK], "mm" if (b == 1 or n < 4) else "tr", "f_acc")
+        def first_products(b, tiles):
+            for n in tiles:
+                acc = bank([P, BANK], "f_acc")
                 cols = slice(P * n, P * (n + 1))
                 for a in range(2):
                     nc.tensor.matmul_mx(
@@ -136,11 +143,14 @@ def tile_list_safari_guide_match_kernel(
 
         w2_c = [[] for q in range(4)]
 
-        def quantise_w2(q, copy):
+        def quantise_w2(q):
             for a in range(2):
-                w2_c[q].append(placed([P, HALF], U32, "w2_c%d_%d" % (q, a), W2_WORK + (4 * q + 2 * a if q < 2 else 4 + 2 * q + a)))
-                grouped = placed([P, HALF, PACK], BF16, "w2_grouped%d_%d" % (q, a), W2_WORK + (12 if q < 2 else -8) + 4 * q + 2 * a)
-                interleave(copy, grouped[:], w2_raw[q][a][:])
+                w2_c[q].append(placed([P, HALF], U32, "w2_c%d_%d" % (q, a), W2_WORK + 2 * (q % 2) + a))
+                grouped = placed([P, HALF, PACK], BF16, "w2_grouped%d_%d" % (q, a), W2_WORK + 4 + 4 * (q in (1, 2)) + 2 * a)
+                if q < 3:
+                    interleave(nc.vector.tensor_copy if q < 2 else nc.scalar.copy, grouped[:], w2_raw[q][a][:])
+                else:
+                    nc.gpsimd.tensor_copy(grouped[:], w2_raw[q][a][:].rearrange("p j c -> p c j"))
                 nc.vector.quantize_mx(
                     out=w2_c[q][a][:].bitcast(FP8X4), scales=w2_s[q][a][:], in_=grouped[:].rearrange("p c j -> p (c j)")
                 )
@@ -149,7 +159,7 @@ def tile_list_safari_guide_match_kernel(
             b, hq = divmod(q, 2)
             part = slice(64 * hq, 64 * (hq + 1))
             for u in range(4):
-                acc = bank([P, 2, HALF], "mm", "s_acc")
+                acc = bank([P, 2, HALF], "s_acc")
                 for n2 in range(2):
                     cols = slice(P * (2 * u + n2), P * (2 * u + n2 + 1))
                     for a in range(2):
@@ -166,7 +176,7 @@ def tile_list_safari_guide_match_kernel(
         def h_tile(b, i):
             h = placed([P, S], F32, "h%d_%d" % (b, i), (H0 if b == 0 else LARGER) + 4 * i)
             for half in range(2):
-                acc = bank([P, 4, P], "tr", "h_acc")
+                acc = bank([P, 4, P], "h_acc")
                 for step, src in enumerate((f_t, m_t)):
                     for nn in range(4):
                         n = 4 * half + nn
@@ -187,9 +197,10 @@ def tile_list_safari_guide_match_kernel(
             nc.vector.quantize_mx(out=codes[:].bitcast(FP8X4), scales=scales[:], in_=grouped[:].rearrange("p c j -> p (c j)"))
             return codes, scales
 
-        first_products(0)
+        first_products(0, range(8))
+        first_products(1, range(4))
         for q in range(2):
-            quantise_w2(q, nc.vector.tensor_copy)
+            quantise_w2(q)
             second_products(q)
         pick2 = placed([P, PACK, NP], F32, "pick2_0", PICKS)
         pick1 = placed([P, PACK, NP], F32, "pick1_0", PICKS + 8)
@@ -201,38 +212,40 @@ def tile_list_safari_guide_match_kernel(
 
         pick_block0(0)
         pick_block0(1)
-        first_products(1)
+        first_products(1, range(4, 8))
         for q in range(2, 4):
-            quantise_w2(q, nc.scalar.copy)
+            quantise_w2(q)
             second_products(q)
         pick_block0(2)
         pick_block0(3)
 
         tab2_w = [placed([P, T3], U32, "tab2_w%d" % a, TABLE + 8 * a) for a in range(2)]
-        tab2_s = placed([P, T3], U8, "tab2_s", W4)
-        nc.gpsimd.memset(tab2_s[:].bitcast(I32), 0)
         for a in range(2):
             load_words(tab2_w[a], tab2_words[a])
+        v2_s = placed([P, S2], U8, "v2_s", W4)
+        nc.gpsimd.memset(v2_s[:].bitcast(I32), 0)
         for quad in range(4):
             for a in range(2):
+                row = 16 * a + 4 * quad
                 nc.sync.dma_start(
-                    out=tab2_s[32 * quad + 4 * a : 32 * quad + 4 * a + 4, :].bitcast(I32),
-                    in_=tab2_scales[a, 4 * quad : 4 * quad + 4, :].bitcast(I32),
+                    out=v2_s[32 * quad + 4 * a : 32 * quad + 4 * a + 4, :].bitcast(I32),
+                    in_=v2_rows[row : row + 4, :].bitcast(I32),
                 )
+        exper_sb = placed([P, S2 // P], F32, "exper_sb", W4 + 2)
+        with nc.allow_non_contiguous_dma(reason="one value of exper for each partition"):
+            nc.sync.dma_start(out=exper_sb[:], in_=exper.rearrange("(c p) -> p c", p=P))
         v2_w = [placed([P, S2], U32, "v2_w%d" % a, FIRST + 2 * a) for a in range(2)]
-        v2_s = placed([P, S2], U8, "v2_s", FIRST + 4)
         for a in range(2):
             nc.vector.tensor_copy(v2_w[a][:], tab2_w[a][:].indirect(offs2_sb[:]))
-        nc.vector.tensor_copy(v2_s[:], tab2_s[:].indirect(offs2_sb[:]))
-
-        x2_0 = quantise_x(pick2, NP, abs_copy, "x2_0", X_WORK, kept([P, NP], U32, "x2_0_c"))
-        x1_0 = quantise_x(pick1, NP, nc.scalar.copy, "x1_0", X_WORK + 4, placed([P, NP], U32, "x1_0_c", X_WORK + 12))
 
         pick2_1 = placed([P, PACK, NP], F32, "pick2_1", TABLE + 16)
         hs = []
         for i in range(PACK):
             hs.append(h_tile(1, i))
             nc.vector.tensor_copy(pick2_1[:, i, :], hs[i][:].indirect(pos2_sb[:]))
+
+        x2_0 = quantise_x(pick2, NP, abs_copy, "x2_0", X_WORK, kept([P, NP], U32, "x2_0_c"))
+        x1_0 = quantise_x(pick1, NP, nc.scalar.copy, "x1_0", X_WORK + 4, placed([P, NP], U32, "x1_0_c", X_WORK + 12))
 
         def guide_pass(acc, c, a, codes, scales, start, stop):
             cols = slice(P * c, P * (c + 1))
@@ -241,10 +254,10 @@ def tile_list_safari_guide_match_kernel(
                 rhs=codes.bitcast(FP8X4), rhs_scale=scales, start=start, stop=stop,
             )
 
-        e2_acc = [bank([P, NP], "mm", "e2_acc") for c in range(4)]
+        e2_acc = [bank([P, NP], "e2_acc") for c in range(4)]
         for c in range(4):
             guide_pass(e2_acc[c][:], c, 0, x2_0[0][:], x2_0[1][:], True, False)
-        e1_acc = [[bank([P, 2, HALF], "tr", "e1_acc") for pair in range(2)] for hf in range(2)]
+        e1_acc = [[bank([P, 2, HALF], "e1_acc") for pair in range(2)] for hf in range(2)]
         for hf in range(2):
             cols = slice(HALF * hf, HALF * (hf + 1))
             for c in range(4):

@@ -59,7 +59,7 @@ def tile_list_safari_guide_match_kernel(
         pos2_sb = kept([P, NP // 16], U16, "pos2_sb")
         tab_s = placed([P, T], U8, "tab_s", TABLE + 16)
         tab_w = [placed([P, T], U32, "tab_w%d" % a, TABLE + 16 * a) for a in range(2)]
-        w4_w = placed([P, 2, 2 * H], U8, "w4_w", W4)
+        w4_w = placed([P, 2, H], U16, "w4_w", W4)
         w4_s = kept([P, 2, H], U8, "w4_s")
         ident = kept([P, P], F32, "ident")
         v_w = [kept([P, S], U32, "v_w%d" % a) for a in range(2)]
@@ -69,7 +69,7 @@ def tile_list_safari_guide_match_kernel(
         v_s = [kept([P, S], U8, "v_s%d" % a) for a in range(2)]
         w2_s = [[kept([P, HALF], U8, "w2_s%d_%d" % (q, a)) for a in range(2)] for q in range(4)]
         f_t = [[placed([P, 2, PACK, P], F32, "f_t%d_%d" % (b, u), FIRST + 16 * b + 4 * u) for u in range(4)] for b in range(2)]
-        m_t = [[placed([P, 2, PACK, P], F32, "m_t%d_%d" % (b, u), LARGER + 16 * b + 4 * u) for u in range(4)] for b in range(2)]
+        m_t = [[placed([P, 2, 2, P], F32, "m_t%d_%d" % (q, u), LARGER + 8 * q + 2 * u) for u in range(4)] for q in range(4)]
 
         nc.gpsimd.memset(w4_s[:].rearrange("p a t -> p (a t)").bitcast(I32), 0)
         for window in (tab_s, tab2_s):
@@ -115,11 +115,11 @@ def tile_list_safari_guide_match_kernel(
         for u in range(4):
             nc.vector.tensor_copy(v_w[1][:, HALF * u : HALF * (u + 1)], tab_w[1][:].indirect(offs_sb[:, 16 * u : 16 * (u + 1)]))
 
-        w2_raw = [[placed([P, PACK, HALF], F32, "w2_raw%d_%d" % (q, a), TABLE + 8 * q + 4 * a) for a in range(2)] for q in range(4)]
-        for q in range(4):
+        w2_raw = [[placed([P, PACK, BANK], F32, "w2_raw%d_%d" % (b, a), TABLE + 16 * b + 8 * a) for a in range(2)] for b in range(2)]
+        for b in range(2):
             for a in range(2):
-                rows = w2[BANK * a : BANK * (a + 1), HALF * q : HALF * (q + 1)]
-                nc.sync.dma_start(out=w2_raw[q][a][:], in_=rows.rearrange("(p j) c -> p j c", j=PACK))
+                rows = w2[BANK * a : BANK * (a + 1), BANK * b : BANK * (b + 1)]
+                nc.sync.dma_start(out=w2_raw[b][a][:], in_=rows.rearrange("(p j) c -> p j c", j=PACK))
 
         def interleave(copy, dst, src):
             copy(dst.rearrange("p (c i) j -> p c j i", i=4), src.rearrange("p j (c i) -> p c j i", i=4))
@@ -128,36 +128,41 @@ def tile_list_safari_guide_match_kernel(
             nc.scalar.activation(out=dst, in_=src, func=ACT.Abs)
 
         def first_products(b, tiles):
+            block = slice(BANK * b, BANK * (b + 1))
             for n in tiles:
                 acc = bank([P, BANK], "f_acc")
                 cols = slice(P * n, P * (n + 1))
                 for a in range(2):
                     nc.tensor.matmul_mx(
                         out=acc[:], lhsT=v_w[a][:, cols].bitcast(FP8X4), lhsT_scale=v_s[a][:, cols],
-                        rhs=w4_w[:, a, 2 * BANK * b : 2 * BANK * (b + 1)].bitcast(FP4X4), rhs_scale=w4_s[:, a, BANK * b : BANK * (b + 1)],
+                        rhs=w4_w[:, a, block].bitcast(FP4X4), rhs_scale=w4_s[:, a, block],
                         start=(a == 0), stop=(a == 1),
                     )
                 nc.scalar.activation(
-                    out=f_t[b][n // 2][:, n % 2, :, :], in_=acc[:].rearrange("p (m t) -> p t m", t=PACK), func=ACT.Copy
+                    out=f_t[b][n // 2][:, n % 2, :, :].rearrange("p t m -> p m t"),
+                    in_=acc[:].rearrange("p (m t) -> p m t", t=PACK), func=ACT.Copy,
                 )
 
-        w2_c = [[] for q in range(4)]
+        w2_c = [[None, None] for q in range(4)]
 
-        def quantise_w2(q):
+        def quantise_w2(b, copy):
             for a in range(2):
-                w2_c[q].append(placed([P, HALF], U32, "w2_c%d_%d" % (q, a), W2_WORK + 2 * (q % 2) + a))
-                grouped = placed([P, HALF, PACK], BF16, "w2_grouped%d_%d" % (q, a), W2_WORK + 4 + 4 * (q in (1, 2)) + 2 * a)
-                if q < 3:
-                    interleave(nc.vector.tensor_copy if q < 2 else nc.scalar.copy, grouped[:], w2_raw[q][a][:])
-                else:
-                    nc.gpsimd.tensor_copy(grouped[:], w2_raw[q][a][:].rearrange("p j c -> p c j"))
-                nc.vector.quantize_mx(
-                    out=w2_c[q][a][:].bitcast(FP8X4), scales=w2_s[q][a][:], in_=grouped[:].rearrange("p c j -> p (c j)")
-                )
+                for pair in range(2):
+                    q = 2 * b + pair
+                    w2_c[q][a] = placed([P, HALF], U32, "w2_c%d_%d" % (q, a), W2_WORK + 2 * pair + a)
+                    grouped = placed([P, 2, P, PACK], BF16, "w2_grouped%d_%d" % (q, a), W2_WORK + 4 + 4 * pair + 2 * a)
+                    copy(
+                        grouped[:].rearrange("p t m j -> p m j t"),
+                        w2_raw[b][a][:].rearrange("p j (m t) -> p m j t", t=PACK)[:, :, :, 2 * pair : 2 * pair + 2],
+                    )
+                    nc.vector.quantize_mx(
+                        out=w2_c[q][a][:].bitcast(FP8X4), scales=w2_s[q][a][:],
+                        in_=grouped[:].rearrange("p t m j -> p (t m j)"),
+                    )
 
         def second_products(q):
-            b, hq = divmod(q, 2)
-            part = slice(64 * hq, 64 * (hq + 1))
+            b, pair = divmod(q, 2)
+            part = slice(2 * pair, 2 * pair + 2)
             for u in range(4):
                 acc = bank([P, 2, HALF], "s_acc")
                 for n2 in range(2):
@@ -169,19 +174,20 @@ def tile_list_safari_guide_match_kernel(
                             start=(a == 0), stop=(a == 1),
                         )
                 nc.vector.tensor_tensor(
-                    out=m_t[b][u][:, :, :, part], in0=acc[:].rearrange("p n (m t) -> p n t m", t=PACK),
-                    in1=f_t[b][u][:, :, :, part], op=ALU.max,
+                    out=m_t[q][u][:].rearrange("p n t m -> p n (t m)"), in0=acc[:],
+                    in1=f_t[b][u][:, :, part, :].rearrange("p n t m -> p n (t m)"), op=ALU.max,
                 )
 
         def h_tile(b, i):
             h = placed([P, S], F32, "h%d_%d" % (b, i), (H0 if b == 0 else LARGER) + 4 * i)
             for half in range(2):
                 acc = bank([P, 4, P], "h_acc")
-                for step, src in enumerate((f_t, m_t)):
+                for step in range(2):
                     for nn in range(4):
-                        n = 4 * half + nn
+                        u, n2 = divmod(4 * half + nn, 2)
+                        src = f_t[b][u][:, n2, i, :] if step == 0 else m_t[2 * b + i // 2][u][:, n2, i % 2, :]
                         nc.tensor.matmul(
-                            acc[:, nn, :], src[b][n // 2][:, n % 2, i, :], ident[:], is_transpose=True,
+                            acc[:, nn, :], src, ident[:], is_transpose=True,
                             start=(step == 0 and nn == 0), stop=(step == 1 and nn == 3),
                         )
                 nc.scalar.activation(
@@ -199,30 +205,25 @@ def tile_list_safari_guide_match_kernel(
 
         first_products(0, range(8))
         first_products(1, range(4))
-        for q in range(2):
-            quantise_w2(q)
-            second_products(q)
+        quantise_w2(0, nc.vector.tensor_copy)
+        second_products(0)
+        second_products(1)
         pick2 = placed([P, PACK, NP], F32, "pick2_0", PICKS)
         pick1 = placed([P, PACK, NP], F32, "pick1_0", PICKS + 8)
-
-        def pick_block0(i):
+        for i in range(PACK):
             h = h_tile(0, i)
             nc.vector.tensor_copy(pick2[:, i, :], h[:].indirect(pos2_sb[:]))
             nc.vector.tensor_copy(pick1[:, i, :], h[:].indirect(pos1_sb[:]))
 
-        pick_block0(0)
-        pick_block0(1)
         first_products(1, range(4, 8))
-        for q in range(2, 4):
-            quantise_w2(q)
-            second_products(q)
-        pick_block0(2)
-        pick_block0(3)
+        quantise_w2(1, nc.scalar.copy)
+        second_products(2)
+        second_products(3)
 
         tab2_w = [placed([P, T3], U32, "tab2_w%d" % a, TABLE + 8 * a) for a in range(2)]
         for a in range(2):
             load_words(tab2_w[a], tab2_words[a])
-        v2_s = placed([P, S2], U8, "v2_s", W4)
+        v2_s = placed([P, S2], U8, "v2_s", W4 + 2)
         nc.gpsimd.memset(v2_s[:].bitcast(I32), 0)
         for quad in range(4):
             for a in range(2):
@@ -231,7 +232,7 @@ def tile_list_safari_guide_match_kernel(
                     out=v2_s[32 * quad + 4 * a : 32 * quad + 4 * a + 4, :].bitcast(I32),
                     in_=v2_rows[row : row + 4, :].bitcast(I32),
                 )
-        exper_sb = placed([P, S2 // P], F32, "exper_sb", W4 + 2)
+        exper_sb = placed([P, S2 // P], F32, "exper_sb", W4 + 3)
         with nc.allow_non_contiguous_dma(reason="one value of exper for each partition"):
             nc.sync.dma_start(out=exper_sb[:], in_=exper.rearrange("(c p) -> p c", p=P))
         v2_w = [placed([P, S2], U32, "v2_w%d" % a, FIRST + 2 * a) for a in range(2)]

from contextlib import ExitStack

import concourse.mybir as mybir
from concourse.masks import make_identity

K, T, S, H, T3, S2, NP = 1024, 4096, 1024, 1024, 2048, 512, 512
FLOPS = 2 * (2 * K * H * S + 2 * H * S2 * NP)

F32 = mybir.dt.float32
BF16 = mybir.dt.bfloat16
I32 = mybir.dt.int32
U32 = mybir.dt.uint32
U16 = mybir.dt.uint16
U8 = mybir.dt.uint8
FP8X4 = mybir.dt.float8_e4m3fn_x4
FP4X4 = mybir.dt.float4_e2m1fn_x4
ALU = mybir.AluOpType
ACT = mybir.ActivationFunctionType

P = 128
PACK = 4
BANK = 512
HALF = 256
KB = 1024

TABLE = 0
W4 = 32
FIRST = 36
LARGER = 68
H0 = 100
W2_WORK = 116
PICKS = 136
X_WORK = 152
ROWS = 168


def tile_list_safari_guide_match_kernel(
    tc, tab_words, tab_scales, offs, tab2_words, tab2_scales, offs2, pos1, pos2,
    w4_words, w4_scales, w2, gain, exper, out,
):
    nc = tc.nc
    with ExitStack() as ctx:
        keep = ctx.enter_context(tc.tile_pool(name="keep", bufs=1))
        shared = ctx.enter_context(tc.tile_pool(name="shared", bufs=1))
        psum = ctx.enter_context(tc.psum_pool(name="psum", bufs=8))

        def kept(shape, dtype, name):
            return keep.tile(shape, dtype, name=name, align_bytes=64)

        def placed(shape, dtype, name, kib):
            return shared.tile(shape, dtype, name=name, offset=kib * KB, align_bytes=64)

        def bank(shape, name):
            return psum.tile(shape, F32, name=name, tag="bank")

        offs_sb = kept([P, S // 16], U16, "offs_sb")
        offs2_sb = kept([P, S2 // 16], U16, "offs2_sb")
        pos1_sb = kept([P, NP // 16], U16, "pos1_sb")
        pos2_sb = kept([P, NP // 16], U16, "pos2_sb")
        tab_s = placed([P, T], U8, "tab_s", TABLE + 16)
        tab_w = [placed([P, T], U32, "tab_w%d" % a, TABLE + 16 * a) for a in range(2)]
        w4_w = placed([P, 2, H], U16, "w4_w", W4)
        w4_s = kept([P, 2, H], U8, "w4_s")
        ident = kept([P, P], F32, "ident")
        v_w = [kept([P, S], U32, "v_w%d" % a) for a in range(2)]
        v_rows = placed([P, S], U8, "v_rows", ROWS)
        tab2_s = kept([P, T3], U8, "tab2_s")
        v2_rows = kept([P, S2], U8, "v2_rows")
        v_s = [kept([P, S], U8, "v_s%d" % a) for a in range(2)]
        w2_s = [[kept([P, HALF], U8, "w2_s%d_%d" % (q, a)) for a in range(2)] for q in range(4)]
        f_t = [[placed([P, 2, PACK, P], F32, "f_t%d_%d" % (b, u), FIRST + 16 * b + 4 * u) for u in range(4)] for b in range(2)]
        m_t = [[placed([P, 2, 2, P], F32, "m_t%d_%d" % (q, u), LARGER + 8 * q + 2 * u) for u in range(4)] for q in range(4)]

        nc.gpsimd.memset(w4_s[:].rearrange("p a t -> p (a t)").bitcast(I32), 0)
        for window in (tab_s, tab2_s):
            nc.vector.memset(window[32:64, :].bitcast(I32), 0)
            nc.vector.memset(window[64:P, :].bitcast(I32), 0)
        for a in range(2):
            nc.vector.memset(v_s[a][:].bitcast(I32), 0)

        def load_words(dst, src):
            nc.sync.dma_start(out=dst[:].bitcast(I32), in_=src.rearrange("p t i -> p (t i)").bitcast(I32))

        nc.sync.dma_start(offs_sb[:], offs)
        nc.sync.dma_start(out=tab_s[0:32, :].bitcast(I32), in_=tab_scales.rearrange("a q t -> (a q) t").bitcast(I32))
        nc.sync.dma_start(offs2_sb[:], offs2)
        nc.sync.dma_start(out=tab2_s[0:32, :].bitcast(I32), in_=tab2_scales.rearrange("a q t -> (a q) t").bitcast(I32))
        nc.sync.dma_start(pos2_sb[:], pos2)
        nc.sync.dma_start(pos1_sb[:], pos1)
        load_words(tab_w[0], tab_words[0])
        nc.sync.dma_start(out=w4_w[:].bitcast(I32), in_=w4_words.rearrange("a p c -> p a c").bitcast(I32))
        for quad in range(4):
            (nc.scalar if quad == 0 else nc.gpsimd).dma_start(
                out=w4_s[32 * quad : 32 * quad + 4, :, :].bitcast(I32),
                in_=w4_scales[:, 4 * quad : 4 * quad + 4, :].rearrange("a r t -> r a t").bitcast(I32),
            )

        nc.vector.tensor_copy(v_rows[:], tab_s[:].indirect(offs_sb[:]))

        def move_scale_rows(a):
            for quad in range(4):
                row = 16 * a + 4 * quad
                nc.sync.dma_start(
                    out=v_s[a][32 * quad : 32 * quad + 4, :].bitcast(I32), in_=v_rows[row : row + 4, :].bitcast(I32)
                )

        move_scale_rows(0)
        load_words(tab_w[1], tab_words[1])
        move_scale_rows(1)
        gain_sb = placed([P, 2, PACK], F32, "gain_sb", ROWS)
        nc.gpsimd.dma_start(out=gain_sb[:], in_=gain.rearrange("(b p i) -> p b i", b=2, i=PACK))
        make_identity(nc, ident[:])
        nc.vector.tensor_copy(v2_rows[:], tab2_s[:].indirect(offs2_sb[:]))
        nc.vector.tensor_copy(v_w[0][:], tab_w[0][:].indirect(offs_sb[:]))
        for u in range(4):
            nc.vector.tensor_copy(v_w[1][:, HALF * u : HALF * (u + 1)], tab_w[1][:].indirect(offs_sb[:, 16 * u : 16 * (u + 1)]))

        w2_raw = [[placed([P, PACK, BANK], F32, "w2_raw%d_%d" % (b, a), TABLE + 16 * b + 8 * a) for a in range(2)] for b in range(2)]
        for b in range(2):
            for a in range(2):
                rows = w2[BANK * a : BANK * (a + 1), BANK * b : BANK * (b + 1)]
                nc.sync.dma_start(out=w2_raw[b][a][:], in_=rows.rearrange("(p j) c -> p j c", j=PACK))

        def interleave(copy, dst, src):
            copy(dst.rearrange("p (c i) j -> p c j i", i=4), src.rearrange("p j (c i) -> p c j i", i=4))

        def abs_copy(dst, src):
            nc.scalar.activation(out=dst, in_=src, func=ACT.Abs)

        def first_products(b, tiles):
            block = slice(BANK * b, BANK * (b + 1))
            for n in tiles:
                acc = bank([P, BANK], "f_acc")
                cols = slice(P * n, P * (n + 1))
                for a in range(2):
                    nc.tensor.matmul_mx(
                        out=acc[:], lhsT=v_w[a][:, cols].bitcast(FP8X4), lhsT_scale=v_s[a][:, cols],
                        rhs=w4_w[:, a, block].bitcast(FP4X4), rhs_scale=w4_s[:, a, block],
                        start=(a == 0), stop=(a == 1),
                    )
                nc.scalar.activation(
                    out=f_t[b][n // 2][:, n % 2, :, :].rearrange("p t m -> p m t"),
                    in_=acc[:].rearrange("p (m t) -> p m t", t=PACK), func=ACT.Copy,
                )

        w2_c = [[None, None] for q in range(4)]

        def quantise_w2(b, copy):
            for a in range(2):
                for pair in range(2):
                    q = 2 * b + pair
                    w2_c[q][a] = placed([P, HALF], U32, "w2_c%d_%d" % (q, a), W2_WORK + 2 * pair + a)
                    grouped = placed([P, 2, P, PACK], BF16, "w2_grouped%d_%d" % (q, a), W2_WORK + 4 + 4 * pair + 2 * a)
                    copy(
                        grouped[:].rearrange("p t m j -> p m j t"),
                        w2_raw[b][a][:].rearrange("p j (m t) -> p m j t", t=PACK)[:, :, :, 2 * pair : 2 * pair + 2],
                    )
                    nc.vector.quantize_mx(
                        out=w2_c[q][a][:].bitcast(FP8X4), scales=w2_s[q][a][:],
                        in_=grouped[:].rearrange("p t m j -> p (t m j)"),
                    )

        def second_products(q):
            b, pair = divmod(q, 2)
            part = slice(2 * pair, 2 * pair + 2)
            for u in range(4):
                acc = bank([P, 2, HALF], "s_acc")
                for n2 in range(2):
                    cols = slice(P * (2 * u + n2), P * (2 * u + n2 + 1))
                    for a in range(2):
                        nc.tensor.matmul_mx(
                            out=acc[:, n2, :], lhsT=v_w[a][:, cols].bitcast(FP8X4), lhsT_scale=v_s[a][:, cols],
                            rhs=w2_c[q][a][:].bitcast(FP8X4), rhs_scale=w2_s[q][a][:],
                            start=(a == 0), stop=(a == 1),
                        )
                nc.vector.tensor_tensor(
                    out=m_t[q][u][:].rearrange("p n t m -> p n (t m)"), in0=acc[:],
                    in1=f_t[b][u][:, :, part, :].rearrange("p n t m -> p n (t m)"), op=ALU.max,
                )

        def h_tile(b, i):
            h = placed([P, S], F32, "h%d_%d" % (b, i), (H0 if b == 0 else LARGER) + 4 * i)
            for half in range(2):
                acc = bank([P, 4, P], "h_acc")
                for step in range(2):
                    for nn in range(4):
                        u, n2 = divmod(4 * half + nn, 2)
                        src = f_t[b][u][:, n2, i, :] if step == 0 else m_t[2 * b + i // 2][u][:, n2, i % 2, :]
                        nc.tensor.matmul(
                            acc[:, nn, :], src, ident[:], is_transpose=True,
                            start=(step == 0 and nn == 0), stop=(step == 1 and nn == 3),
                        )
                nc.scalar.activation(
                    out=h[:, BANK * half : BANK * (half + 1)], in_=acc[:].rearrange("p n c -> p (n c)"),
                    func=ACT.Copy, scale=gain_sb[:, b, i : i + 1],
                )
            return h

        def quantise_x(picked, width, copy, name, grouped_at, codes):
            grouped = placed([P, width, PACK], BF16, name + "_grouped", grouped_at)
            interleave(copy, grouped[:], picked[:])
            scales = kept([P, width], U8, name + "_s")
            nc.vector.quantize_mx(out=codes[:].bitcast(FP8X4), scales=scales[:], in_=grouped[:].rearrange("p c j -> p (c j)"))
            return codes, scales

        first_products(0, range(8))
        first_products(1, range(4))
        quantise_w2(0, nc.vector.tensor_copy)
        second_products(0)
        second_products(1)
        pick2 = placed([P, PACK, NP], F32, "pick2_0", PICKS)
        pick1 = placed([P, PACK, NP], F32, "pick1_0", PICKS + 8)
        for i in range(PACK):
            h = h_tile(0, i)
            nc.vector.tensor_copy(pick2[:, i, :], h[:].indirect(pos2_sb[:]))
            nc.vector.tensor_copy(pick1[:, i, :], h[:].indirect(pos1_sb[:]))

        first_products(1, range(4, 8))
        quantise_w2(1, nc.scalar.copy)
        second_products(2)
        second_products(3)

        tab2_w = [placed([P, T3], U32, "tab2_w%d" % a, TABLE + 8 * a) for a in range(2)]
        for a in range(2):
            load_words(tab2_w[a], tab2_words[a])
        v2_s = placed([P, S2], U8, "v2_s", W4 + 2)
        nc.gpsimd.memset(v2_s[:].bitcast(I32), 0)
        for quad in range(4):
            for a in range(2):
                row = 16 * a + 4 * quad
                nc.sync.dma_start(
                    out=v2_s[32 * quad + 4 * a : 32 * quad + 4 * a + 4, :].bitcast(I32),
                    in_=v2_rows[row : row + 4, :].bitcast(I32),
                )
        exper_sb = placed([P, S2 // P], F32, "exper_sb", W4 + 3)
        with nc.allow_non_contiguous_dma(reason="one value of exper for each partition"):
            nc.sync.dma_start(out=exper_sb[:], in_=exper.rearrange("(c p) -> p c", p=P))
        v2_w = [placed([P, S2], U32, "v2_w%d" % a, FIRST + 2 * a) for a in range(2)]
        for a in range(2):
            nc.vector.tensor_copy(v2_w[a][:], tab2_w[a][:].indirect(offs2_sb[:]))

        pick2_1 = placed([P, PACK, NP], F32, "pick2_1", TABLE + 16)
        hs = []
        for i in range(PACK):
            hs.append(h_tile(1, i))
            nc.vector.tensor_copy(pick2_1[:, i, :], hs[i][:].indirect(pos2_sb[:]))

        x2_0 = quantise_x(pick2, NP, abs_copy, "x2_0", X_WORK, kept([P, NP], U32, "x2_0_c"))
        x1_0 = quantise_x(pick1, NP, nc.scalar.copy, "x1_0", X_WORK + 4, placed([P, NP], U32, "x1_0_c", X_WORK + 12))

        def guide_pass(acc, c, a, codes, scales, start, stop):
            cols = slice(P * c, P * (c + 1))
            nc.tensor.matmul_mx(
                out=acc, lhsT=v2_w[a][:, cols].bitcast(FP8X4), lhsT_scale=v2_s[4 * a : P, cols],
                rhs=codes.bitcast(FP8X4), rhs_scale=scales, start=start, stop=stop,
            )

        e2_acc = [bank([P, NP], "e2_acc") for c in range(4)]
        for c in range(4):
            guide_pass(e2_acc[c][:], c, 0, x2_0[0][:], x2_0[1][:], True, False)
        e1_acc = [[bank([P, 2, HALF], "e1_acc") for pair in range(2)] for hf in range(2)]
        for hf in range(2):
            cols = slice(HALF * hf, HALF * (hf + 1))
            for c in range(4):
                guide_pass(e1_acc[hf][c // 2][:, c % 2, :], c, 0, x1_0[0][:, cols], x1_0[1][:, cols], c % 2 == 0, False)

        x2_1 = quantise_x(pick2_1, NP, abs_copy, "x2_1", X_WORK + 8, kept([P, NP], U32, "x2_1_c"))
        e2 = placed([P, 4, NP], F32, "e2", FIRST + 8)
        for c in range(4):
            guide_pass(e2_acc[c][:], c, 1, x2_1[0][:], x2_1[1][:], False, True)
            nc.scalar.activation(out=e2[:, c, :], in_=e2_acc[c][:], func=ACT.Copy, scale=exper_sb[:, c : c + 1])

        for hf in range(2):
            cols = slice(HALF * hf, HALF * (hf + 1))
            pick1_1 = placed([P, PACK, HALF], F32, "pick1_1_%d" % hf, X_WORK + 12 - 4 * hf)
            for i in range(PACK):
                nc.vector.tensor_copy(pick1_1[:, i, :], hs[i][:].indirect(pos1_sb[:, 16 * hf : 16 * (hf + 1)]))
            x1_1 = quantise_x(
                pick1_1, HALF, nc.scalar.copy if hf == 0 else nc.vector.tensor_copy, "x1_1_%d" % hf,
                X_WORK + 2 * hf, kept([P, HALF], U32, "x1_1_c%d" % hf),
            )
            for pair in range(2):
                acc = e1_acc[hf][pair]
                for c2 in range(2):
                    guide_pass(acc[:, c2, :], 2 * pair + c2, 1, x1_1[0][:], x1_1[1][:], False, c2 == 1)
                res = placed([P, 2, HALF], F32, "res%d_%d" % (hf, pair), FIRST + 16 + 4 * hf + 2 * pair)
                nc.vector.tensor_tensor(out=res[:], in0=acc[:], in1=e2[:, 2 * pair : 2 * pair + 2, cols], op=ALU.mult)
                rows = out[HALF * pair : HALF * (pair + 1), cols]
                nc.sync.dma_start(out=rows.rearrange("(c p) j -> p c j", p=P), in_=res[:])
